import numpy as np
import ml_dtypes


def mxq(x, axis, fmt="e4m3"):
    dtype, down = {"e4m3": (ml_dtypes.float8_e4m3fn, 7), "e5m2": (ml_dtypes.float8_e5m2, 14)}[fmt]
    v = np.moveaxis(np.asarray(x, np.float32).astype(ml_dtypes.bfloat16).astype(np.float64), axis, -1)
    blocks = v.reshape(v.shape[:-1] + (-1, 32))
    amax = np.abs(blocks).max(-1, keepdims=True)
    byte = np.maximum(np.where(amax > 0, np.frexp(amax)[1] - 1 + 127, 0) - down, 1)
    scale = np.exp2(byte - 127.0)
    codes = (blocks / scale).astype(np.float32).astype(dtype).astype(np.float64)
    return np.moveaxis((codes * scale).reshape(v.shape), -1, axis)


WIDE = False


def mx_kscale(k):
    if not WIDE:
        return np.ones(k)
    levels = np.array([30, -30])
    if k % 512:
        return np.exp2(np.random.permutation(np.resize(levels, k // 32))).repeat(32)
    a = np.empty((k // 512, 16))
    for p in range(k // 512):
        a[p, :8] = np.random.permutation(np.resize(levels, 8))
        for g in range(8):
            far = levels[np.abs(levels - a[p, g]) >= 10]
            a[p, g + 8] = far[np.random.randint(len(far))]
    return np.exp2(a.ravel()).repeat(32)


def f64(x):
    return np.asarray(x).astype(np.float64)


def striped(idx):
    return np.tile(np.asarray(idx).reshape(-1, 16).T, (8, 1)).astype(np.uint16)


def unstriped(offs):
    return offs[:16].T.reshape(-1).astype(np.int64)


E2M1 = np.array([0.0, 0.5, 1.0, 1.5, 2.0, 3.0, 4.0, 6.0, -0.0, -0.5, -1.0, -1.5, -2.0, -3.0, -4.0, -6.0])


def pack_weight(w, fmt):
    k, n = w.shape
    w = f64(np.asarray(w, np.float32).astype(ml_dtypes.bfloat16)).reshape(k // 32, 32, n)
    amax = np.abs(w).max(1)
    if fmt in ("e4m3", "e5m2"):
        byte = np.frexp(amax)[1] - 1 + 127 - (7 if fmt == "e4m3" else 14)
    else:
        mant, ex = np.frexp(amax / 6.0)
        byte = np.where(mant > 0.5, ex, ex - 1) + 127
    byte = np.clip(np.where(amax > 0, byte, 1), 1, 254)
    scaled = (w * np.exp2(127.0 - byte)[:, None, :]).reshape(k, n).astype(np.float32)
    by_word = np.ascontiguousarray(scaled.reshape(k // 512, 128, 4, n).transpose(0, 1, 3, 2))
    if fmt in ("e4m3", "e5m2"):
        words = by_word.astype(ml_dtypes.float8_e4m3fn if fmt == "e4m3" else ml_dtypes.float8_e5m2).view(np.uint8)
    else:
        c = by_word.astype(ml_dtypes.float4_e2m1fn).view(np.uint8) & 0xF
        words = (c[..., 0::2] | (c[..., 1::2] << 4)).reshape(k // 512, 128, 2 * n)
    return np.ascontiguousarray(words), np.ascontiguousarray(byte.astype(np.uint8).reshape(k // 512, 16, n))


def unpack_weight(words, scales, fmt):
    g, _, n = scales.shape
    words = np.ascontiguousarray(words).reshape(g, 128, n, -1)
    if fmt in ("e4m3", "e5m2"):
        vals = words.view(ml_dtypes.float8_e4m3fn if fmt == "e4m3" else ml_dtypes.float8_e5m2).astype(np.float64)
    else:
        nib = np.empty((g, 128, n, 4), np.uint8)
        nib[..., 0::2] = words & 0xF
        nib[..., 1::2] = words >> 4
        vals = E2M1[nib]
    vals = vals * np.repeat(np.exp2(scales.astype(np.float64) - 127.0), 8, axis=1)[..., None]
    return vals.transpose(0, 1, 3, 2).reshape(g * 512, n)


K, T, J, R, V, O, N, E = 512, 1024, 256, 512, 1024, 128, 256, 512


def setup_inputs():
    n = np.random.standard_normal
    idx = np.random.permutation(V)[:R]
    idx2 = np.random.permutation(T)[:J]
    idx3 = np.random.permutation(J)[:O]
    idx4 = np.random.permutation(J)[:O]
    idx5 = np.random.permutation(E)[:O]
    idx6 = np.random.permutation(E)[:O]
    fk = mx_kscale(K)
    fr = mx_kscale(R)
    tr = np.ones(V)
    tr[idx] = fr
    xtp = pack_weight(n((K, T)) / fk[:, None], "e2m1")
    wtp = pack_weight(n((K, V)) * 1 / np.sqrt(K) * fk[:, None] * tr, "e5m2")
    w2p = pack_weight(n((K, R)) * 1 / np.sqrt(K) * fk[:, None], "e4m3")
    wbp = pack_weight(n((R, N)) * 1 / np.sqrt(R) / fr[:, None], "e4m3")
    return {
        "xt_words": xtp[0],
        "xt_scales": xtp[1],
        "wt_words": wtp[0],
        "wt_scales": wtp[1],
        "w2_words": w2p[0],
        "w2_scales": w2p[1],
        "wb_words": wbp[0],
        "wb_scales": wbp[1],
        "offs": striped(idx),
        "offs2": striped(idx2),
        "offs3": striped(idx3),
        "offs4": striped(idx4),
        "offs5": striped(idx5),
        "offs6": striped(idx6),
    }


def reference(xt_words, xt_scales, wt_words, wt_scales, w2_words, w2_scales, wb_words, wb_scales, offs, offs2, offs3, offs4, offs5, offs6):
    idx = unstriped(offs)
    idx2 = unstriped(offs2)
    idx3 = unstriped(offs3)
    idx4 = unstriped(offs4)
    idx5 = unstriped(offs5)
    idx6 = unstriped(offs6)
    xtu = unpack_weight(xt_words, xt_scales, "e2m1")
    wtu = unpack_weight(wt_words, wt_scales, "e5m2")
    w2u = unpack_weight(w2_words, w2_scales, "e4m3")
    wbu = unpack_weight(wb_words, wb_scales, "e4m3")
    wtidxg = wtu[:, idx]
    xtidx2g = xtu[:, idx2]
    a = wtidxg.T @ xtidx2g
    b = w2u.T @ xtidx2g
    lb = b[:, 0:1]
    la = a[:, 0:1]
    hid = np.abs(a[:, idx3] * lb - b[:, idx4] * la)
    hidq = mxq(hid, 0, "e5m2")
    p = wbu.T @ hidq
    pa = np.zeros((N, E))
    pa[:, idx5] = p
    pb = np.zeros((N, E))
    pb[:, idx6] = p
    y = pa + pb
    return y

@@ -1,0 +1,168 @@
+from contextlib import ExitStack
+
+import concourse.mybir as mybir
+
+K, T, J, R, V, O, N, E = 512, 1024, 256, 512, 1024, 128, 256, 512
+FLOPS = 2 * K * R * J * 2 + 2 * R * N * O
+
+F32 = mybir.dt.float32
+BF16 = mybir.dt.bfloat16
+I32 = mybir.dt.int32
+U32 = mybir.dt.uint32
+U16 = mybir.dt.uint16
+U8 = mybir.dt.uint8
+E4M3X4 = mybir.dt.float8_e4m3fn_x4
+E5M2X4 = mybir.dt.float8_e5m2_x4
+E2M1X4 = mybir.dt.float4_e2m1fn_x4
+ACT = mybir.ActivationFunctionType
+ALU = mybir.AluOpType
+
+P = 128
+PACK = 4
+HALF = O // 2
+
+
+def load_scales(queues, plane, scales):
+    rows = scales[0].bitcast(I32)
+    width = rows.shape[1]
+    for q in range(4):
+        src = rows[4 * q:4 * q + 4, :].unsqueeze(0).broadcast_to([8, 4, width])
+        queues[q].dma_start(out=plane[32 * q:32 * q + 32, :].bitcast(I32), in_=src)
+
+
+def tile_list_leadboth_storeleads_one_pagetwice_kernel(
+    tc, xt_words, xt_scales, wt_words, wt_scales, w2_words, w2_scales, wb_words, wb_scales,
+    offs, offs2, offs3, offs4, offs5, offs6, out,
+):
+    nc = tc.nc
+    with ExitStack() as ctx:
+        keep = ctx.enter_context(tc.tile_pool(name="keep", bufs=1))
+        psum = ctx.enter_context(tc.psum_pool(name="psum", bufs=8))
+
+        def sb(name, shape, dtype):
+            return keep.tile(shape, dtype, name=name, align_bytes=64)
+
+        idx = sb("idx", [P, R // 16], U16)
+        idx2 = sb("idx2", [P, J // 16], U16)
+        idx3 = sb("idx3", [P, O // 16], U16)
+        idx4 = sb("idx4", [P, O // 16], U16)
+        idx5 = sb("idx5", [P, O // 16], U16)
+        idx6 = sb("idx6", [P, O // 16], U16)
+        xt_w = sb("xt_w", [P, T], U16)
+        xt_s = sb("xt_s", [P, T], U8)
+        wt_w = sb("wt_w", [P, V], U32)
+        wt_s = sb("wt_s", [P, V], U8)
+        w2_w = sb("w2_w", [P, R], U32)
+        w2_s = sb("w2_s", [P, R], U8)
+        wb_w = sb("wb_w", [P, N], U32)
+        wb_s = sb("wb_s", [P, N], U8)
+
+        def words(ap):
+            return ap[0].rearrange("p c r -> p (c r)").bitcast(I32)
+
+        nc.sync.dma_start(idx[:], offs)
+        load_scales([nc.sync, nc.sync, nc.scalar, nc.scalar], wt_s, wt_scales)
+        nc.sync.dma_start(idx2[:], offs2)
+        nc.scalar.dma_start(out=xt_w[:].bitcast(I32), in_=xt_words[0].bitcast(I32))
+        nc.scalar.dma_start(out=wt_w[:].bitcast(I32), in_=words(wt_words))
+        load_scales([nc.sync, nc.sync, nc.scalar, nc.scalar], xt_s, xt_scales)
+        nc.sync.dma_start(out=w2_w[:].bitcast(I32), in_=words(w2_words))
+        load_scales([nc.sync, nc.sync, nc.gpsimd, nc.gpsimd], w2_s, w2_scales)
+        nc.sync.dma_start(idx3[:], offs3)
+        nc.sync.dma_start(idx4[:], offs4)
+        nc.sync.dma_start(out=wb_w[:].bitcast(I32), in_=words(wb_words))
+        load_scales([nc.sync] * 4, wb_s, wb_scales)
+        nc.sync.dma_start(idx5[:], offs5)
+        nc.sync.dma_start(idx6[:], offs6)
+
+        pa = [sb(f"pa{h}", [P, E], F32) for h in range(2)]
+        pb = [sb(f"pb{h}", [P, E], F32) for h in range(2)]
+        for page in pa + pb:
+            nc.vector.memset(page[:], 0.0)
+
+        xg_w = sb("xg_w", [P, J], U16)
+        xg_s = sb("xg_s", [P, J], U8)
+        wg_w = sb("wg_w", [P, R], U32)
+        wg_s = sb("wg_s", [P, R], U8)
+        w2d_w = sb("w2d_w", [P, R], U32)
+        w2d_s = sb("w2d_s", [P, R], U8)
+
+        def dealt(tile):
+            return tile[:].rearrange("p (t q) -> p q t", t=PACK)
+
+        nc.vector.tensor_copy(out=dealt(wg_s), in_=wt_s[:].indirect(idx[:]))
+        nc.vector.tensor_copy(out=xg_w[:], in_=xt_w[:].indirect(idx2[:]))
+        nc.vector.tensor_copy(out=xg_s[:], in_=xt_s[:].indirect(idx2[:]))
+        nc.vector.tensor_copy(out=dealt(wg_w), in_=wt_w[:].indirect(idx[:]))
+
+        for dst, src in ((w2d_w, w2_w), (w2d_s, w2_s)):
+            nc.gpsimd.tensor_copy(
+                out=dst[:].rearrange("p (t q) -> p t q", t=PACK),
+                in_=src[:].rearrange("p (q t) -> p t q", t=PACK),
+            )
+
+        def first_product(w_words, w_scales, fmt, t):
+            acc = psum.tile([P, J], F32, name="acc")
+            cols = slice(t * P, (t + 1) * P)
+            nc.tensor.matmul_mx(
+                out=acc[:], lhsT=w_words[:, cols].bitcast(fmt), lhsT_scale=w_scales[:, cols],
+                rhs=xg_w[:].bitcast(E2M1X4), rhs_scale=xg_s[:], start=True, stop=True,
+            )
+            return acc
+
+        a = [sb(f"a{t}", [P, J], F32) for t in range(PACK)]
+        b = [sb(f"b{t}", [P, J], F32) for t in range(PACK)]
+        def b_rows(t):
+            acc = first_product(w2d_w, w2d_s, E4M3X4, t)
+            if t < 2:
+                nc.scalar.activation(out=b[t][:], in_=acc[:], func=ACT.Copy)
+            else:
+                nc.vector.tensor_copy(out=b[t][:], in_=acc[:])
+
+        def a_rows(t):
+            acc = first_product(wg_w, wg_s, E5M2X4, t)
+            nc.vector.tensor_copy(out=a[t][:], in_=acc[:])
+
+        b_rows(0)
+        b_rows(1)
+        a_rows(0)
+        a_rows(1)
+        for t in (2, 3):
+            b_rows(t)
+            a_rows(t)
+        hid_w = sb("hid_w", [P, O], U32)
+        hid_s = sb("hid_s", [P, O], U8)
+        u = sb("u", [P, PACK, O], F32)
+        v = sb("v", [P, PACK, O], F32)
+        d = sb("d", [P, PACK, O], F32)
+        for t in range(PACK):
+            nc.scalar.activation(out=u[:, t, :], in_=a[t][:].indirect(idx3[:]), func=ACT.Copy, scale=b[t][:, 0:1])
+            nc.scalar.activation(out=v[:, t, :], in_=b[t][:].indirect(idx4[:]), func=ACT.Copy, scale=a[t][:, 0:1])
+            nc.vector.tensor_tensor(out=d[:, t, :], in0=u[:, t, :], in1=v[:, t, :], op=ALU.subtract)
+        hid = sb("hid", [P, O, PACK], BF16)
+        nc.scalar.activation(
+            out=hid[:].rearrange("p (c i) t -> p c t i", i=4),
+            in_=d[:].rearrange("p t (c i) -> p c t i", i=4),
+            func=ACT.Abs,
+        )
+        nc.vector.quantize_mx(out=hid_w[:].bitcast(E5M2X4), scales=hid_s[:], in_=hid[:].rearrange("p o t -> p (o t)"))
+        p = []
+        for h in range(2):
+            acc = psum.tile([P, O], F32, name="acc")
+            cols = slice(h * P, (h + 1) * P)
+            nc.tensor.matmul_mx(
+                out=acc[:], lhsT=wb_w[:, cols].bitcast(E4M3X4), lhsT_scale=wb_s[:, cols],
+                rhs=hid_w[:].bitcast(E5M2X4), rhs_scale=hid_s[:], start=True, stop=True,
+            )
+            rows = sb(f"p{h}", [P, O], F32)
+            if h == 0:
+                nc.vector.tensor_copy(out=rows[:], in_=acc[:])
+            else:
+                nc.scalar.copy(out=rows[:], in_=acc[:])
+            p.append(rows)
+        for h in range(2):
+            nc.vector.tensor_copy(out=pa[h][:].indirect(idx5[:]), in_=p[h][:])
+            nc.scalar.activation(out=pb[h][:].indirect(idx6[:]), in_=p[h][:], func=ACT.Copy)
+            y = sb(f"y{h}", [P, E], F32)
+            nc.vector.tensor_tensor(out=y[:], in0=pa[h][:], in1=pb[h][:], op=ALU.add)
+            nc.sync.dma_start(out=out[h * P:(h + 1) * P, :], in_=y[:])

@@ -95,12 +95,14 @@ def tile_list_leadboth_storeleads_one_pagetwice_kernel(
         nc.vector.tensor_copy(out=xg_s[:], in_=xt_s[:].indirect(idx2[:]))
         nc.vector.tensor_copy(out=dealt(wg_w), in_=wt_w[:].indirect(idx[:]))
 
-        for dst, src in ((w2d_w, w2_w), (w2d_s, w2_s)):
-            nc.gpsimd.tensor_copy(
+        def deal(copy, dst, src):
+            copy(
                 out=dst[:].rearrange("p (t q) -> p t q", t=PACK),
                 in_=src[:].rearrange("p (q t) -> p t q", t=PACK),
             )
 
+        deal(nc.scalar.copy, w2d_w, w2_w)
+        deal(nc.vector.tensor_copy, w2d_s, w2_s)
         def first_product(w_words, w_scales, fmt, t):
             acc = psum.tile([P, J], F32, name="acc")
             cols = slice(t * P, (t + 1) * P)
@@ -112,24 +114,11 @@ def tile_list_leadboth_storeleads_one_pagetwice_kernel(
 
         a = [sb(f"a{t}", [P, J], F32) for t in range(PACK)]
         b = [sb(f"b{t}", [P, J], F32) for t in range(PACK)]
-        def b_rows(t):
+        for t in range(PACK):
             acc = first_product(w2d_w, w2d_s, E4M3X4, t)
-            if t < 2:
-                nc.scalar.activation(out=b[t][:], in_=acc[:], func=ACT.Copy)
-            else:
-                nc.vector.tensor_copy(out=b[t][:], in_=acc[:])
-
-        def a_rows(t):
+            nc.vector.tensor_copy(out=b[t][:], in_=acc[:])
             acc = first_product(wg_w, wg_s, E5M2X4, t)
             nc.vector.tensor_copy(out=a[t][:], in_=acc[:])
-
-        b_rows(0)
-        b_rows(1)
-        a_rows(0)
-        a_rows(1)
-        for t in (2, 3):
-            b_rows(t)
-            a_rows(t)
         hid_w = sb("hid_w", [P, O], U32)
         hid_s = sb("hid_s", [P, O], U8)
         u = sb("u", [P, PACK, O], F32)
@@ -163,6 +152,9 @@ def tile_list_leadboth_storeleads_one_pagetwice_kernel(
         for h in range(2):
             nc.vector.tensor_copy(out=pa[h][:].indirect(idx5[:]), in_=p[h][:])
             nc.scalar.activation(out=pb[h][:].indirect(idx6[:]), in_=p[h][:], func=ACT.Copy)
-            y = sb(f"y{h}", [P, E], F32)
-            nc.vector.tensor_tensor(out=y[:], in0=pa[h][:], in1=pb[h][:], op=ALU.add)
-            nc.sync.dma_start(out=out[h * P:(h + 1) * P, :], in_=y[:])
+            pieces = 1 if h == 0 else 2
+            for c in range(pieces):
+                cols = slice(c * E // pieces, (c + 1) * E // pieces)
+                y = sb(f"y{h}{c}", [P, E // pieces], F32)
+                nc.vector.tensor_tensor(out=y[:], in0=pa[h][:, cols], in1=pb[h][:, cols], op=ALU.add)
+                nc.sync.dma_start(out=out[h * P:(h + 1) * P, cols], in_=y[:])

@@ -68,8 +68,8 @@ def tile_list_leadboth_storeleads_one_pagetwice_kernel(
         load_scales([nc.sync, nc.sync, nc.scalar, nc.scalar], xt_s, xt_scales)
         nc.sync.dma_start(out=w2_w[:].bitcast(I32), in_=words(w2_words))
         load_scales([nc.sync, nc.sync, nc.gpsimd, nc.gpsimd], w2_s, w2_scales)
-        nc.sync.dma_start(idx3[:], offs3)
         nc.sync.dma_start(idx4[:], offs4)
+        nc.sync.dma_start(idx3[:], offs3)
         nc.sync.dma_start(out=wb_w[:].bitcast(I32), in_=words(wb_words))
         load_scales([nc.sync] * 4, wb_s, wb_scales)
         nc.sync.dma_start(idx5[:], offs5)
@@ -95,14 +95,12 @@ def tile_list_leadboth_storeleads_one_pagetwice_kernel(
         nc.vector.tensor_copy(out=xg_s[:], in_=xt_s[:].indirect(idx2[:]))
         nc.vector.tensor_copy(out=dealt(wg_w), in_=wt_w[:].indirect(idx[:]))
 
-        def deal(copy, dst, src):
-            copy(
-                out=dst[:].rearrange("p (t q) -> p t q", t=PACK),
-                in_=src[:].rearrange("p (q t) -> p t q", t=PACK),
-            )
-
-        deal(nc.scalar.copy, w2d_w, w2_w)
-        deal(nc.vector.tensor_copy, w2d_s, w2_s)
+        nc.scalar.copy(
+            out=w2d_w[:].rearrange("p (t q) -> p t q", t=PACK),
+            in_=w2_w[:].rearrange("p (q t) -> p t q", t=PACK),
+        )
+        for t in range(PACK):
+            nc.vector.tensor_copy(out=w2d_s[:, t * P:(t + 1) * P], in_=w2_s[:, t::PACK])
         def first_product(w_words, w_scales, fmt, t):
             acc = psum.tile([P, J], F32, name="acc")
             cols = slice(t * P, (t + 1) * P)
@@ -114,24 +112,32 @@ def tile_list_leadboth_storeleads_one_pagetwice_kernel(
 
         a = [sb(f"a{t}", [P, J], F32) for t in range(PACK)]
         b = [sb(f"b{t}", [P, J], F32) for t in range(PACK)]
+        la0 = sb("la0", [P, 1], F32)
         for t in range(PACK):
             acc = first_product(w2d_w, w2d_s, E4M3X4, t)
             nc.vector.tensor_copy(out=b[t][:], in_=acc[:])
             acc = first_product(wg_w, wg_s, E5M2X4, t)
+            if t == 0:
+                nc.vector.tensor_copy(out=la0[:], in_=acc[:, 0:1])
             nc.vector.tensor_copy(out=a[t][:], in_=acc[:])
+        la = [la0[:]] + [a[t][:, 0:1] for t in range(1, PACK)]
         hid_w = sb("hid_w", [P, O], U32)
         hid_s = sb("hid_s", [P, O], U8)
         u = sb("u", [P, PACK, O], F32)
         v = sb("v", [P, PACK, O], F32)
         d = sb("d", [P, PACK, O], F32)
         for t in range(PACK):
+            nc.scalar.activation(out=v[:, t, :], in_=b[t][:].indirect(idx4[:]), func=ACT.Copy, scale=la[t])
             nc.scalar.activation(out=u[:, t, :], in_=a[t][:].indirect(idx3[:]), func=ACT.Copy, scale=b[t][:, 0:1])
-            nc.scalar.activation(out=v[:, t, :], in_=b[t][:].indirect(idx4[:]), func=ACT.Copy, scale=a[t][:, 0:1])
             nc.vector.tensor_tensor(out=d[:, t, :], in0=u[:, t, :], in1=v[:, t, :], op=ALU.subtract)
         hid = sb("hid", [P, O, PACK], BF16)
+        d_low = d[:, :, 0:HALF].rearrange("p t o -> p o t")
+        nc.vector.scalar_tensor_tensor(
+            out=hid[:, 0:HALF, :], in0=d_low, scalar=-1.0, in1=d_low, op0=ALU.mult, op1=ALU.max,
+        )
         nc.scalar.activation(
-            out=hid[:].rearrange("p (c i) t -> p c t i", i=4),
-            in_=d[:].rearrange("p t (c i) -> p c t i", i=4),
+            out=hid[:, HALF:O, :].rearrange("p (c i) t -> p c t i", i=4),
+            in_=d[:, :, HALF:O].rearrange("p t (c i) -> p c t i", i=4),
             func=ACT.Abs,
         )
         nc.vector.quantize_mx(out=hid_w[:].bitcast(E5M2X4), scales=hid_s[:], in_=hid[:].rearrange("p o t -> p (o t)"))
@@ -152,9 +158,9 @@ def tile_list_leadboth_storeleads_one_pagetwice_kernel(
         for h in range(2):
             nc.vector.tensor_copy(out=pa[h][:].indirect(idx5[:]), in_=p[h][:])
             nc.scalar.activation(out=pb[h][:].indirect(idx6[:]), in_=p[h][:], func=ACT.Copy)
-            pieces = 1 if h == 0 else 2
-            for c in range(pieces):
-                cols = slice(c * E // pieces, (c + 1) * E // pieces)
-                y = sb(f"y{h}{c}", [P, E // pieces], F32)
+        for h in range(2):
+            for c in range(2):
+                cols = slice(c * E // 2, (c + 1) * E // 2)
+                y = sb(f"y{h}{c}", [P, E // 2], F32)
                 nc.vector.tensor_tensor(out=y[:], in0=pa[h][:, cols], in1=pb[h][:, cols], op=ALU.add)
                 nc.sync.dma_start(out=out[h * P:(h + 1) * P, cols], in_=y[:])

from contextlib import ExitStack

import concourse.mybir as mybir

K, T, J, R, V, O, N, E = 512, 1024, 256, 512, 1024, 128, 256, 512
FLOPS = 2 * K * R * J * 2 + 2 * R * N * O

F32 = mybir.dt.float32
BF16 = mybir.dt.bfloat16
I32 = mybir.dt.int32
U32 = mybir.dt.uint32
U16 = mybir.dt.uint16
U8 = mybir.dt.uint8
E4M3X4 = mybir.dt.float8_e4m3fn_x4
E5M2X4 = mybir.dt.float8_e5m2_x4
E2M1X4 = mybir.dt.float4_e2m1fn_x4
ACT = mybir.ActivationFunctionType
ALU = mybir.AluOpType

P = 128
PACK = 4
HALF = O // 2


def load_scales(queues, plane, scales):
    rows = scales[0].bitcast(I32)
    width = rows.shape[1]
    for q in range(4):
        src = rows[4 * q:4 * q + 4, :].unsqueeze(0).broadcast_to([8, 4, width])
        queues[q].dma_start(out=plane[32 * q:32 * q + 32, :].bitcast(I32), in_=src)


def tile_list_leadboth_storeleads_one_pagetwice_kernel(
    tc, xt_words, xt_scales, wt_words, wt_scales, w2_words, w2_scales, wb_words, wb_scales,
    offs, offs2, offs3, offs4, offs5, offs6, out,
):
    nc = tc.nc
    with ExitStack() as ctx:
        keep = ctx.enter_context(tc.tile_pool(name="keep", bufs=1))
        psum = ctx.enter_context(tc.psum_pool(name="psum", bufs=8))

        def sb(name, shape, dtype):
            return keep.tile(shape, dtype, name=name, align_bytes=64)

        idx = sb("idx", [P, R // 16], U16)
        idx2 = sb("idx2", [P, J // 16], U16)
        idx3 = sb("idx3", [P, O // 16], U16)
        idx4 = sb("idx4", [P, O // 16], U16)
        idx5 = sb("idx5", [P, O // 16], U16)
        idx6 = sb("idx6", [P, O // 16], U16)
        xt_w = sb("xt_w", [P, T], U16)
        xt_s = sb("xt_s", [P, T], U8)
        wt_w = sb("wt_w", [P, V], U32)
        wt_s = sb("wt_s", [P, V], U8)
        w2_w = sb("w2_w", [P, R], U32)
        w2_s = sb("w2_s", [P, R], U8)
        wb_w = sb("wb_w", [P, N], U32)
        wb_s = sb("wb_s", [P, N], U8)

        def words(ap):
            return ap[0].rearrange("p c r -> p (c r)").bitcast(I32)

        nc.sync.dma_start(idx[:], offs)
        load_scales([nc.sync, nc.sync, nc.scalar, nc.scalar], wt_s, wt_scales)
        nc.sync.dma_start(idx2[:], offs2)
        nc.scalar.dma_start(out=xt_w[:].bitcast(I32), in_=xt_words[0].bitcast(I32))
        nc.scalar.dma_start(out=wt_w[:].bitcast(I32), in_=words(wt_words))
        load_scales([nc.sync, nc.sync, nc.scalar, nc.scalar], xt_s, xt_scales)
        nc.sync.dma_start(out=w2_w[:].bitcast(I32), in_=words(w2_words))
        load_scales([nc.sync, nc.sync, nc.gpsimd, nc.gpsimd], w2_s, w2_scales)
        nc.sync.dma_start(idx4[:], offs4)
        nc.sync.dma_start(idx3[:], offs3)
        nc.sync.dma_start(out=wb_w[:].bitcast(I32), in_=words(wb_words))
        load_scales([nc.sync] * 4, wb_s, wb_scales)
        nc.sync.dma_start(idx5[:], offs5)
        nc.sync.dma_start(idx6[:], offs6)

        pa = [sb(f"pa{h}", [P, E], F32) for h in range(2)]
        pb = [sb(f"pb{h}", [P, E], F32) for h in range(2)]
        for page in pa + pb:
            nc.vector.memset(page[:], 0.0)

        xg_w = sb("xg_w", [P, J], U16)
        xg_s = sb("xg_s", [P, J], U8)
        wg_w = sb("wg_w", [P, R], U32)
        wg_s = sb("wg_s", [P, R], U8)
        w2d_w = sb("w2d_w", [P, R], U32)
        w2d_s = sb("w2d_s", [P, R], U8)

        def dealt(tile):
            return tile[:].rearrange("p (t q) -> p q t", t=PACK)

        nc.vector.tensor_copy(out=dealt(wg_s), in_=wt_s[:].indirect(idx[:]))
        nc.vector.tensor_copy(out=xg_w[:], in_=xt_w[:].indirect(idx2[:]))
        nc.vector.tensor_copy(out=xg_s[:], in_=xt_s[:].indirect(idx2[:]))
        nc.vector.tensor_copy(out=dealt(wg_w), in_=wt_w[:].indirect(idx[:]))

        nc.scalar.copy(
            out=w2d_w[:].rearrange("p (t q) -> p t q", t=PACK),
            in_=w2_w[:].rearrange("p (q t) -> p t q", t=PACK),
        )
        for t in range(PACK):
            nc.vector.tensor_copy(out=w2d_s[:, t * P:(t + 1) * P], in_=w2_s[:, t::PACK])
        def first_product(w_words, w_scales, fmt, t):
            acc = psum.tile([P, J], F32, name="acc")
            cols = slice(t * P, (t + 1) * P)
            nc.tensor.matmul_mx(
                out=acc[:], lhsT=w_words[:, cols].bitcast(fmt), lhsT_scale=w_scales[:, cols],
                rhs=xg_w[:].bitcast(E2M1X4), rhs_scale=xg_s[:], start=True, stop=True,
            )
            return acc

        a = [sb(f"a{t}", [P, J], F32) for t in range(PACK)]
        b = [sb(f"b{t}", [P, J], F32) for t in range(PACK)]
        la0 = sb("la0", [P, 1], F32)
        for t in range(PACK):
            acc = first_product(w2d_w, w2d_s, E4M3X4, t)
            nc.vector.tensor_copy(out=b[t][:], in_=acc[:])
            acc = first_product(wg_w, wg_s, E5M2X4, t)
            if t == 0:
                nc.vector.tensor_copy(out=la0[:], in_=acc[:, 0:1])
            nc.vector.tensor_copy(out=a[t][:], in_=acc[:])
        la = [la0[:]] + [a[t][:, 0:1] for t in range(1, PACK)]
        hid_w = sb("hid_w", [P, O], U32)
        hid_s = sb("hid_s", [P, O], U8)
        u = sb("u", [P, PACK, O], F32)
        v = sb("v", [P, PACK, O], F32)
        d = sb("d", [P, PACK, O], F32)
        for t in range(PACK):
            nc.scalar.activation(out=v[:, t, :], in_=b[t][:].indirect(idx4[:]), func=ACT.Copy, scale=la[t])
            nc.scalar.activation(out=u[:, t, :], in_=a[t][:].indirect(idx3[:]), func=ACT.Copy, scale=b[t][:, 0:1])
            nc.vector.tensor_tensor(out=d[:, t, :], in0=u[:, t, :], in1=v[:, t, :], op=ALU.subtract)
        hid = sb("hid", [P, O, PACK], BF16)
        d_low = d[:, :, 0:HALF].rearrange("p t o -> p o t")
        nc.vector.scalar_tensor_tensor(
            out=hid[:, 0:HALF, :], in0=d_low, scalar=-1.0, in1=d_low, op0=ALU.mult, op1=ALU.max,
        )
        nc.scalar.activation(
            out=hid[:, HALF:O, :].rearrange("p (c i) t -> p c t i", i=4),
            in_=d[:, :, HALF:O].rearrange("p t (c i) -> p c t i", i=4),
            func=ACT.Abs,
        )
        nc.vector.quantize_mx(out=hid_w[:].bitcast(E5M2X4), scales=hid_s[:], in_=hid[:].rearrange("p o t -> p (o t)"))
        p = []
        for h in range(2):
            acc = psum.tile([P, O], F32, name="acc")
            cols = slice(h * P, (h + 1) * P)
            nc.tensor.matmul_mx(
                out=acc[:], lhsT=wb_w[:, cols].bitcast(E4M3X4), lhsT_scale=wb_s[:, cols],
                rhs=hid_w[:].bitcast(E5M2X4), rhs_scale=hid_s[:], start=True, stop=True,
            )
            rows = sb(f"p{h}", [P, O], F32)
            if h == 0:
                nc.vector.tensor_copy(out=rows[:], in_=acc[:])
            else:
                nc.scalar.copy(out=rows[:], in_=acc[:])
            p.append(rows)
        for h in range(2):
            nc.vector.tensor_copy(out=pa[h][:].indirect(idx5[:]), in_=p[h][:])
            nc.scalar.activation(out=pb[h][:].indirect(idx6[:]), in_=p[h][:], func=ACT.Copy)
        for h in range(2):
            for c in range(2):
                cols = slice(c * E // 2, (c + 1) * E // 2)
                y = sb(f"y{h}{c}", [P, E // 2], F32)
                nc.vector.tensor_tensor(out=y[:], in0=pa[h][:, cols], in1=pb[h][:, cols], op=ALU.add)
                nc.sync.dma_start(out=out[h * P:(h + 1) * P, cols], in_=y[:])
